import numpy as np
import ml_dtypes


def mxq(x, axis, fmt="e4m3"):
    dtype, down = {"e4m3": (ml_dtypes.float8_e4m3fn, 7), "e5m2": (ml_dtypes.float8_e5m2, 14)}[fmt]
    v = np.moveaxis(np.asarray(x, np.float32).astype(ml_dtypes.bfloat16).astype(np.float64), axis, -1)
    blocks = v.reshape(v.shape[:-1] + (-1, 32))
    amax = np.abs(blocks).max(-1, keepdims=True)
    byte = np.maximum(np.where(amax > 0, np.frexp(amax)[1] - 1 + 127, 0) - down, 1)
    scale = np.exp2(byte - 127.0)
    codes = (blocks / scale).astype(np.float32).astype(dtype).astype(np.float64)
    return np.moveaxis((codes * scale).reshape(v.shape), -1, axis)


WIDE = False


def mx_kscale(k):
    if not WIDE:
        return np.ones(k)
    levels = np.array([10, -10, 5, -5, 0])
    if k % 512:
        return np.exp2(np.random.permutation(np.resize(levels, k // 32))).repeat(32)
    a = np.empty((k // 512, 16))
    for p in range(k // 512):
        a[p, :8] = np.random.permutation(np.resize(levels, 8))
        for g in range(8):
            far = levels[np.abs(levels - a[p, g]) >= 10]
            a[p, g + 8] = far[np.random.randint(len(far))]
    return np.exp2(a.ravel()).repeat(32)


def f64(x):
    return np.asarray(x).astype(np.float64)


def striped(idx):
    return np.tile(np.asarray(idx).reshape(-1, 16).T, (8, 1)).astype(np.uint16)


def unstriped(offs):
    return offs[:16].T.reshape(-1).astype(np.int64)


def bf(x):
    return np.asarray(x, np.float32).astype(ml_dtypes.bfloat16)


def planes(Y):
    r, m = Y.shape
    b = f64(bf(Y)).reshape(r // 32, 32, m)
    amax = np.abs(b).max(1)
    byte = np.clip(np.where(amax > 0, np.frexp(amax)[1] - 1 + 127 - 7, 1), 1, 254)
    codes = (b * np.exp2(127.0 - byte)[:, None, :]).reshape(r, m).astype(np.float32).astype(ml_dtypes.float8_e4m3fn).view(np.uint8)
    words = codes.reshape(r // 512, 128, 4, m).transpose(0, 1, 3, 2)
    return np.ascontiguousarray(words), np.ascontiguousarray(byte.astype(np.uint8).reshape(r // 512, 16, m))


D, T, I, Q, E = 512, 2048, 512, 256, 512


def setup_inputs():
    n = np.random.standard_normal
    idx = np.random.permutation(T)[:I]
    fd = mx_kscale(D)
    fi = mx_kscale(I)
    ti = np.ones(T)
    ti[idx] = fi
    return {
        "query": (n((D, Q)) * 0.4 / np.sqrt(D) * fd[:, None]).astype(np.float32),
        "keys": (n((D, T)) / fd[:, None]).astype(np.float32),
        "size": (np.random.uniform(0.5, 2.0, (1, I)) * fi).astype(np.float32),
        "vals": (n((E, T)) / ti).astype(np.float32),
        "offs": striped(idx),
    }


def reference(query, keys, size, vals, offs):
    idx = unstriped(offs)
    km = f64(keys)[:, idx] - np.mean(f64(keys)[:, idx], axis=1, keepdims=True)
    queryq = mxq(f64(query), 0, "e4m3")
    kmq = mxq(km, 0, "e4m3")
    a = queryq.T @ kmq
    p = np.exp(a - np.max(a, axis=1, keepdims=True))
    w = p * f64(size) / np.sum(p, axis=1, keepdims=True)
    wt = w.T
    vt = f64(vals)[:, idx].T
    vtq = mxq(vt, 0, "e4m3")
    wtq = mxq(wt, 0, "e4m3")
    o = vtq.T @ wtq
    words, scales = planes(o)
    return o, words, scales

@@ -1,0 +1,233 @@
+from contextlib import ExitStack
+
+import concourse.mybir as mybir
+from concourse.masks import make_identity
+
+D, T, I, Q, E = 512, 2048, 512, 256, 512
+FLOPS = 2 * D * I * Q + 2 * I * E * Q
+
+F32 = mybir.dt.float32
+BF16 = mybir.dt.bfloat16
+I32 = mybir.dt.int32
+U32 = mybir.dt.uint32
+U16 = mybir.dt.uint16
+U8 = mybir.dt.uint8
+FP8X4 = mybir.dt.float8_e4m3fn_x4
+ACT = mybir.ActivationFunctionType
+ALU = mybir.AluOpType
+AX = mybir.AxisListType
+
+P = 128
+PACK = 4
+HALVES = Q // P
+KEY_ORDER = (2, 0, 1, 3)
+
+
+def tile_attend_smoothkeys_pl_kernel(tc, query, keys, size, vals, offs, out_0, out_1, out_2):
+    nc = tc.nc
+    with ExitStack() as ctx:
+        sb = ctx.enter_context(tc.tile_pool(name="sb", bufs=1))
+        ps = ctx.enter_context(tc.psum_pool(name="ps", bufs=1))
+
+        def tile(shape, dtype, name, slot=None):
+            return sb.tile(shape, dtype, name=name, tag=slot or name, align_bytes=64)
+
+        def mx_tiles(name, words, slot=None):
+            return tile([P, words], U32, name + "_codes", slot), tile([P, words], U8, name + "_scales")
+
+        def quantise(mx, cols, src):
+            nc.vector.quantize_mx(out=mx[0][:, cols].bitcast(FP8X4), scales=mx[1][:, cols], in_=src)
+
+        def product(out, stationary, s_cols, moving, m_cols):
+            nc.tensor.matmul_mx(
+                out=out,
+                lhsT=stationary[0][:, s_cols].bitcast(FP8X4),
+                lhsT_scale=stationary[1][:, s_cols],
+                rhs=moving[0][:, m_cols].bitcast(FP8X4),
+                rhs_scale=moving[1][:, m_cols],
+                start=True,
+                stop=True,
+            )
+
+        def block(n):
+            return slice(n * P, (n + 1) * P)
+
+        def woven(src):
+            return src.rearrange("p t (c i) -> p c t i", i=4)
+
+        def weave_into(dst):
+            return dst.rearrange("p (c i) t -> p c t i", i=4)
+
+        key_rows = keys.rearrange("(p t) n -> p t n", t=PACK)
+        val_rows = vals.rearrange("(p j) n -> p j n", j=PACK)
+        out_rows = out_0.rearrange("(p j) q -> p j q", j=PACK)
+
+        key_pool = [tile([P, T], F32, "key_pool%d" % t) for t in range(PACK)]
+        val_pool = [tile([P, T], F32, "val_pool%d" % j) for j in range(PACK)]
+        offsets = sb.tile([P, I // 16], U16, name="offsets")
+        q_raw = tile([P, PACK, Q], F32, "q_raw")
+        size_cols = tile([P, PACK], F32, "size_cols")
+
+        nc.sync.dma_start(out=key_pool[KEY_ORDER[0]][:], in_=key_rows[:, KEY_ORDER[0], :])
+        nc.sync.dma_start(offsets[:], offs)
+        for t in KEY_ORDER[1:]:
+            nc.sync.dma_start(out=key_pool[t][:], in_=key_rows[:, t, :])
+        nc.sync.dma_start(out=q_raw[:], in_=query.rearrange("(p t) q -> p t q", t=PACK))
+        for j in range(PACK):
+            nc.sync.dma_start(out=val_pool[j][:], in_=val_rows[:, j, :])
+        nc.scalar.dma_start(out=size_cols[:], in_=size.rearrange("o (s r) -> (o s) r", r=PACK))
+
+        ident = tile([P, P], F32, "ident")
+        make_identity(nc, ident[:])
+        warm = tile([P, 1], F32, "warm")
+        nc.scalar.activation(out=warm[:], in_=ident[:, 0:1], func=ACT.Exp)
+
+        size_ps = ps.tile([P, PACK, P], F32, name="size_ps", tag="turn0")
+        for r in range(PACK):
+            nc.tensor.transpose(size_ps[:, r, :], size_cols[:, r : r + 1].to_broadcast([P, P]), ident[:])
+        size_all = tile([P, I], F32, "size_all")
+        nc.scalar.copy(
+            out=size_all[:].rearrange("p (u s e) -> p u s e", u=2, e=2), in_=size_ps[:].rearrange("p (u e) s -> p u s e", e=2)
+        )
+
+        km = tile([P, I, PACK], BF16, "km")
+
+        def gather_keys(t):
+            picked = tile([P, I], F32, "picked%d" % t)
+            nc.vector.tensor_copy(out=picked[:], in_=key_pool[t][:].indirect(offsets[:]))
+            return picked
+
+        def scaled_sum_on_scalar(t, picked, scale):
+            scaled = tile([P, I], BF16, "scaled%d" % t)
+            total = tile([P, 1], F32, "total%d" % t)
+            nc.scalar.activation(out=scaled[:], in_=picked[:], func=ACT.Copy, scale=scale, accum_out=total[:])
+            return total
+
+        def centre_on_vector(t, picked, neg_mean):
+            nc.vector.tensor_scalar(out=km[:, :, t], in0=picked[:], scalar1=neg_mean[:], scalar2=None, op0=ALU.add)
+
+        first, second, third, last = KEY_ORDER
+        picked_first = gather_keys(first)
+        total_first = scaled_sum_on_scalar(first, picked_first, 1.0)
+        for t in (second, third):
+            picked = gather_keys(t)
+            neg_mean = scaled_sum_on_scalar(t, picked, -1.0 / I)
+            nc.scalar.activation(out=km[:, :, t], in_=picked[:], func=ACT.Identity, bias=neg_mean[:])
+            if t == second:
+                neg_mean_first = tile([P, 1], F32, "neg_mean_first", "key_pool%d" % second)
+                nc.gpsimd.tensor_scalar(
+                    out=neg_mean_first[:], in0=total_first[:], scalar1=-1.0 / I, scalar2=0.0, op0=ALU.mult, op1=ALU.add
+                )
+                centre_on_vector(first, picked_first, neg_mean_first)
+        picked_last = gather_keys(last)
+        scaled_last = tile([P, I], BF16, "scaled_last")
+        neg_mean_last = tile([P, 1], F32, "neg_mean_last")
+        nc.vector.tensor_scalar(
+            out=scaled_last[:], in0=picked_last[:], scalar1=-1.0 / I, scalar2=None, op0=ALU.mult, op1=ALU.add, accum_out=neg_mean_last[:]
+        )
+        centre_on_vector(last, picked_last, neg_mean_last)
+
+        q_bf = [tile([P, P, PACK], BF16, "q_bf%d" % h, ("picked%d" % third, None)[h]) for h in range(HALVES)]
+        for h in range(HALVES):
+            nc.scalar.copy(out=weave_into(q_bf[h][:]), in_=woven(q_raw[:, :, block(h)]))
+        q_mx = [mx_tiles("q%d" % h, P, ("picked%d" % last, None)[h]) for h in range(HALVES)]
+        k_mx = mx_tiles("k", I)
+        everything = slice(None)
+        quantise(q_mx[0], everything, q_bf[0][:].rearrange("p q t -> p (q t)"))
+        quantise(k_mx, everything, km[:].rearrange("p i t -> p (i t)"))
+        quantise(q_mx[1], everything, q_bf[1][:].rearrange("p q t -> p (q t)"))
+
+        scores = [ps.tile([P, I], F32, name="scores%d" % h, tag="scores%d" % h) for h in range(HALVES)]
+        for h in range(HALVES):
+            product(scores[h][:], q_mx[h], everything, k_mx, everything)
+
+        def gather_values(j, slot):
+            vg = tile([P, I], BF16, "vg%d" % j, slot)
+            nc.vector.tensor_copy(out=vg[:], in_=val_pool[j][:].indirect(offsets[:]))
+            return vg
+
+        def turn(src_words, bank, name, dst):
+            turned = ps.tile([P, 2, P], F32, name=name, tag=bank)
+            for u in range(2):
+                nc.tensor.transpose(turned[:, u, :], src_words[u], ident[:])
+            nc.scalar.copy(out=dst.bitcast(F32).rearrange("p (c u) -> p c u", u=2), in_=turned[:].rearrange("p u c -> p c u"))
+
+        def turn_values(j, vg, dst):
+            words = vg[:].bitcast(F32)
+            turn([words[:, u : 2 * P : 2] for u in range(2)], "vt%d" % (j % 2), "vt_ps%d" % j, dst)
+
+        row_sums = tile([P, HALVES], F32, "row_sums")
+
+        def exp_rows(h):
+            neg_max = tile([P, 1], F32, "neg_max%d" % h, ("val_pool0", None)[h])
+            nc.vector.tensor_reduce(out=neg_max[:], in_=scores[h][:], axis=AX.X, op=ALU.max, negate=True)
+            p = tile([P, I], F32, "p%d" % h)
+            nc.scalar.activation(
+                out=p[:].rearrange("p (u s e) -> p u s e", u=2, e=2),
+                in_=scores[h][:].rearrange("p (s u e) -> p u s e", u=2, e=2),
+                func=ACT.Exp,
+                bias=neg_max[:],
+                accum_out=row_sums[:, h : h + 1],
+            )
+            return p
+
+        width = P * PACK
+        vt01 = tile([P, 2 * width], BF16, "vt01")
+        vt2 = tile([P, width], BF16, "vt2")
+        vt3 = tile([P, width], BF16, "vt3")
+        wt = tile([P, HALVES * width], BF16, "wt")
+
+        vg0 = gather_values(0, "km")
+        p_rows = [exp_rows(h) for h in range(HALVES)]
+        turn_values(0, vg0, vt01[:, 0:width])
+        vg1 = gather_values(1, None)
+        inv = tile([P, HALVES], F32, "inv", "val_pool1")
+        nc.vector.reciprocal(out=inv[:], in_=row_sums[:])
+        turn_values(1, vg1, vt01[:, width : 2 * width])
+        for h in range(HALVES):
+            w = tile([P, I], BF16, "w%d" % h)
+            nc.vector.scalar_tensor_tensor(
+                out=w[:], in0=p_rows[h][:], scalar=inv[:, h : h + 1], in1=size_all[:], op0=ALU.mult, op1=ALU.mult
+            )
+            words = w[:].bitcast(F32)
+            turn([words[:, block(u)] for u in range(2)], "turn%d" % h, "wt_ps%d" % h, wt[:, h * width : (h + 1) * width])
+        vg2 = gather_values(2, "p1")
+        vg3 = gather_values(3, None)
+        turn_values(2, vg2, vt2[:])
+        turn_values(3, vg3, vt3[:])
+        w_mx = mx_tiles("w", Q, "val_pool3")
+        quantise(w_mx, everything, wt[:])
+        v01_mx = mx_tiles("v01", 2 * P, "wt")
+        quantise(v01_mx, everything, vt01[:])
+        v2_mx = mx_tiles("v2", P, "vt01")
+        quantise(v2_mx, everything, vt2[:])
+        v3_mx = mx_tiles("v3", P)
+        quantise(v3_mx, everything, vt3[:])
+
+        result = tile([P, PACK, Q], F32, "result")
+        acc01 = ps.tile([P, 2, Q], F32, name="acc01", tag="scores0")
+        for j in range(2):
+            product(acc01[:, j, :], v01_mx, block(j), w_mx, everything)
+        acc2 = ps.tile([P, Q], F32, name="acc2", tag="scores1")
+        product(acc2[:], v2_mx, everything, w_mx, everything)
+        acc3 = [ps.tile([P, P], F32, name="acc3_%d" % h) for h in range(HALVES)]
+        for h in range(HALVES):
+            product(acc3[h][:], v3_mx, everything, w_mx, block(h))
+        nc.scalar.copy(out=result[:, 0:2, :], in_=acc01[:])
+        nc.sync.dma_start(out=out_rows[:, 0:2, :], in_=result[:, 0:2, :])
+        nc.vector.tensor_copy(out=result[:, 2, :], in_=acc2[:])
+        nc.vector.tensor_copy(out=result[:, 3, block(0)], in_=acc3[0][:])
+        nc.scalar.copy(out=result[:, 3, block(1)], in_=acc3[1][:])
+        nc.sync.dma_start(out=out_rows[:, 2:4, :], in_=result[:, 2:4, :])
+
+        y_bf = [tile([P, P, PACK], BF16, "y_bf%d" % h) for h in range(HALVES)]
+        nc.vector.tensor_copy(out=weave_into(y_bf[0][:]), in_=woven(result[:, :, block(0)]))
+        nc.scalar.copy(out=weave_into(y_bf[1][:]), in_=woven(result[:, :, block(1)]))
+        y_mx = mx_tiles("y", Q)
+        for h in range(HALVES):
+            quantise(y_mx, block(h), y_bf[h][:].rearrange("p q j -> p (q j)"))
+        nc.sync.dma_start(out=out_1[0].rearrange("p c r -> p (c r)").bitcast(I32), in_=y_mx[0][:].bitcast(I32))
+        scale_rows = out_2[0].bitcast(I32)
+        for g in range(4):
+            queue = nc.scalar if g % 2 == 0 else nc.sync
+            queue.dma_start(out=scale_rows[4 * g : 4 * g + 4, :], in_=y_mx[1][32 * g : 32 * g + 4, :].bitcast(I32))

@@ -159,9 +159,9 @@ def tile_attend_smoothkeys_pl_kernel(tc, query, keys, size, vals, offs, out_0, o
         row_sums = tile([P, HALVES], F32, "row_sums")
 
         def exp_rows(h):
-            neg_max = tile([P, 1], F32, "neg_max%d" % h, ("val_pool0", None)[h])
+            neg_max = tile([P, 1], F32, "neg_max%d" % h)
             nc.vector.tensor_reduce(out=neg_max[:], in_=scores[h][:], axis=AX.X, op=ALU.max, negate=True)
-            p = tile([P, I], F32, "p%d" % h)
+            p = tile([P, I], F32, "p%d" % h, ("val_pool0", None)[h])
             nc.scalar.activation(
                 out=p[:].rearrange("p (u s e) -> p u s e", u=2, e=2),
                 in_=scores[h][:].rearrange("p (s u e) -> p u s e", u=2, e=2),
@@ -177,10 +177,12 @@ def tile_attend_smoothkeys_pl_kernel(tc, query, keys, size, vals, offs, out_0, o
         vt3 = tile([P, width], BF16, "vt3")
         wt = tile([P, HALVES * width], BF16, "wt")
 
-        vg0 = gather_values(0, "km")
+        val_pool0_bf = tile([P, T], BF16, "val_pool0_bf")
+        nc.scalar.activation(out=val_pool0_bf[:], in_=val_pool[0][:], func=ACT.Copy)
         p_rows = [exp_rows(h) for h in range(HALVES)]
-        turn_values(0, vg0, vt01[:, 0:width])
         vg1 = gather_values(1, None)
+        vg0 = tile([P, I], BF16, "vg0", "neg_max1")
+        nc.scalar.activation(out=vg0[:], in_=val_pool0_bf[:].indirect(offsets[:]), func=ACT.Copy)
         inv = tile([P, HALVES], F32, "inv", "val_pool1")
         nc.vector.reciprocal(out=inv[:], in_=row_sums[:])
         turn_values(1, vg1, vt01[:, width : 2 * width])
@@ -191,7 +193,8 @@ def tile_attend_smoothkeys_pl_kernel(tc, query, keys, size, vals, offs, out_0, o
             )
             words = w[:].bitcast(F32)
             turn([words[:, block(u)] for u in range(2)], "turn%d" % h, "wt_ps%d" % h, wt[:, h * width : (h + 1) * width])
-        vg2 = gather_values(2, "p1")
+        turn_values(0, vg0, vt01[:, 0:width])
+        vg2 = gather_values(2, None)
         vg3 = gather_values(3, None)
         turn_values(2, vg2, vt2[:])
         turn_values(3, vg3, vt3[:])

from contextlib import ExitStack

import concourse.mybir as mybir
from concourse.masks import make_identity

D, T, I, Q, E = 512, 2048, 512, 256, 512
FLOPS = 2 * D * I * Q + 2 * I * E * Q

F32 = mybir.dt.float32
BF16 = mybir.dt.bfloat16
I32 = mybir.dt.int32
U32 = mybir.dt.uint32
U16 = mybir.dt.uint16
U8 = mybir.dt.uint8
FP8X4 = mybir.dt.float8_e4m3fn_x4
ACT = mybir.ActivationFunctionType
ALU = mybir.AluOpType
AX = mybir.AxisListType

P = 128
PACK = 4
HALVES = Q // P
KEY_ORDER = (2, 0, 1, 3)


def tile_attend_smoothkeys_pl_kernel(tc, query, keys, size, vals, offs, out_0, out_1, out_2):
    nc = tc.nc
    with ExitStack() as ctx:
        sb = ctx.enter_context(tc.tile_pool(name="sb", bufs=1))
        ps = ctx.enter_context(tc.psum_pool(name="ps", bufs=1))

        def tile(shape, dtype, name, slot=None):
            return sb.tile(shape, dtype, name=name, tag=slot or name, align_bytes=64)

        def mx_tiles(name, words, slot=None):
            return tile([P, words], U32, name + "_codes", slot), tile([P, words], U8, name + "_scales")

        def quantise(mx, cols, src):
            nc.vector.quantize_mx(out=mx[0][:, cols].bitcast(FP8X4), scales=mx[1][:, cols], in_=src)

        def product(out, stationary, s_cols, moving, m_cols):
            nc.tensor.matmul_mx(
                out=out,
                lhsT=stationary[0][:, s_cols].bitcast(FP8X4),
                lhsT_scale=stationary[1][:, s_cols],
                rhs=moving[0][:, m_cols].bitcast(FP8X4),
                rhs_scale=moving[1][:, m_cols],
                start=True,
                stop=True,
            )

        def block(n):
            return slice(n * P, (n + 1) * P)

        def woven(src):
            return src.rearrange("p t (c i) -> p c t i", i=4)

        def weave_into(dst):
            return dst.rearrange("p (c i) t -> p c t i", i=4)

        key_rows = keys.rearrange("(p t) n -> p t n", t=PACK)
        val_rows = vals.rearrange("(p j) n -> p j n", j=PACK)
        out_rows = out_0.rearrange("(p j) q -> p j q", j=PACK)

        key_pool = [tile([P, T], F32, "key_pool%d" % t) for t in range(PACK)]
        val_pool = [tile([P, T], F32, "val_pool%d" % j) for j in range(PACK)]
        offsets = sb.tile([P, I // 16], U16, name="offsets")
        q_raw = tile([P, PACK, Q], F32, "q_raw")
        size_cols = tile([P, PACK], F32, "size_cols")

        nc.sync.dma_start(out=key_pool[KEY_ORDER[0]][:], in_=key_rows[:, KEY_ORDER[0], :])
        nc.sync.dma_start(offsets[:], offs)
        for t in KEY_ORDER[1:]:
            nc.sync.dma_start(out=key_pool[t][:], in_=key_rows[:, t, :])
        nc.sync.dma_start(out=q_raw[:], in_=query.rearrange("(p t) q -> p t q", t=PACK))
        for j in range(PACK):
            nc.sync.dma_start(out=val_pool[j][:], in_=val_rows[:, j, :])
        nc.scalar.dma_start(out=size_cols[:], in_=size.rearrange("o (s r) -> (o s) r", r=PACK))

        ident = tile([P, P], F32, "ident")
        make_identity(nc, ident[:])
        warm = tile([P, 1], F32, "warm")
        nc.scalar.activation(out=warm[:], in_=ident[:, 0:1], func=ACT.Exp)

        size_ps = ps.tile([P, PACK, P], F32, name="size_ps", tag="turn0")
        for r in range(PACK):
            nc.tensor.transpose(size_ps[:, r, :], size_cols[:, r : r + 1].to_broadcast([P, P]), ident[:])
        size_all = tile([P, I], F32, "size_all")
        nc.scalar.copy(
            out=size_all[:].rearrange("p (u s e) -> p u s e", u=2, e=2), in_=size_ps[:].rearrange("p (u e) s -> p u s e", e=2)
        )

        km = tile([P, I, PACK], BF16, "km")

        def gather_keys(t):
            picked = tile([P, I], F32, "picked%d" % t)
            nc.vector.tensor_copy(out=picked[:], in_=key_pool[t][:].indirect(offsets[:]))
            return picked

        def scaled_sum_on_scalar(t, picked, scale):
            scaled = tile([P, I], BF16, "scaled%d" % t)
            total = tile([P, 1], F32, "total%d" % t)
            nc.scalar.activation(out=scaled[:], in_=picked[:], func=ACT.Copy, scale=scale, accum_out=total[:])
            return total

        def centre_on_vector(t, picked, neg_mean):
            nc.vector.tensor_scalar(out=km[:, :, t], in0=picked[:], scalar1=neg_mean[:], scalar2=None, op0=ALU.add)

        first, second, third, last = KEY_ORDER
        picked_first = gather_keys(first)
        total_first = scaled_sum_on_scalar(first, picked_first, 1.0)
        for t in (second, third):
            picked = gather_keys(t)
            neg_mean = scaled_sum_on_scalar(t, picked, -1.0 / I)
            nc.scalar.activation(out=km[:, :, t], in_=picked[:], func=ACT.Identity, bias=neg_mean[:])
            if t == second:
                neg_mean_first = tile([P, 1], F32, "neg_mean_first", "key_pool%d" % second)
                nc.gpsimd.tensor_scalar(
                    out=neg_mean_first[:], in0=total_first[:], scalar1=-1.0 / I, scalar2=0.0, op0=ALU.mult, op1=ALU.add
                )
                centre_on_vector(first, picked_first, neg_mean_first)
        picked_last = gather_keys(last)
        scaled_last = tile([P, I], BF16, "scaled_last")
        neg_mean_last = tile([P, 1], F32, "neg_mean_last")
        nc.vector.tensor_scalar(
            out=scaled_last[:], in0=picked_last[:], scalar1=-1.0 / I, scalar2=None, op0=ALU.mult, op1=ALU.add, accum_out=neg_mean_last[:]
        )
        centre_on_vector(last, picked_last, neg_mean_last)

        q_bf = [tile([P, P, PACK], BF16, "q_bf%d" % h, ("picked%d" % third, None)[h]) for h in range(HALVES)]
        for h in range(HALVES):
            nc.scalar.copy(out=weave_into(q_bf[h][:]), in_=woven(q_raw[:, :, block(h)]))
        q_mx = [mx_tiles("q%d" % h, P, ("picked%d" % last, None)[h]) for h in range(HALVES)]
        k_mx = mx_tiles("k", I)
        everything = slice(None)
        quantise(q_mx[0], everything, q_bf[0][:].rearrange("p q t -> p (q t)"))
        quantise(k_mx, everything, km[:].rearrange("p i t -> p (i t)"))
        quantise(q_mx[1], everything, q_bf[1][:].rearrange("p q t -> p (q t)"))

        scores = [ps.tile([P, I], F32, name="scores%d" % h, tag="scores%d" % h) for h in range(HALVES)]
        for h in range(HALVES):
            product(scores[h][:], q_mx[h], everything, k_mx, everything)

        def gather_values(j, slot):
            vg = tile([P, I], BF16, "vg%d" % j, slot)
            nc.vector.tensor_copy(out=vg[:], in_=val_pool[j][:].indirect(offsets[:]))
            return vg

        def turn(src_words, bank, name, dst):
            turned = ps.tile([P, 2, P], F32, name=name, tag=bank)
            for u in range(2):
                nc.tensor.transpose(turned[:, u, :], src_words[u], ident[:])
            nc.scalar.copy(out=dst.bitcast(F32).rearrange("p (c u) -> p c u", u=2), in_=turned[:].rearrange("p u c -> p c u"))

        def turn_values(j, vg, dst):
            words = vg[:].bitcast(F32)
            turn([words[:, u : 2 * P : 2] for u in range(2)], "vt%d" % (j % 2), "vt_ps%d" % j, dst)

        row_sums = tile([P, HALVES], F32, "row_sums")

        def exp_rows(h):
            neg_max = tile([P, 1], F32, "neg_max%d" % h)
            nc.vector.tensor_reduce(out=neg_max[:], in_=scores[h][:], axis=AX.X, op=ALU.max, negate=True)
            p = tile([P, I], F32, "p%d" % h, ("val_pool0", None)[h])
            nc.scalar.activation(
                out=p[:].rearrange("p (u s e) -> p u s e", u=2, e=2),
                in_=scores[h][:].rearrange("p (s u e) -> p u s e", u=2, e=2),
                func=ACT.Exp,
                bias=neg_max[:],
                accum_out=row_sums[:, h : h + 1],
            )
            return p

        width = P * PACK
        vt01 = tile([P, 2 * width], BF16, "vt01")
        vt2 = tile([P, width], BF16, "vt2")
        vt3 = tile([P, width], BF16, "vt3")
        wt = tile([P, HALVES * width], BF16, "wt")

        val_pool0_bf = tile([P, T], BF16, "val_pool0_bf")
        nc.scalar.activation(out=val_pool0_bf[:], in_=val_pool[0][:], func=ACT.Copy)
        p_rows = [exp_rows(h) for h in range(HALVES)]
        vg1 = gather_values(1, None)
        vg0 = tile([P, I], BF16, "vg0", "neg_max1")
        nc.scalar.activation(out=vg0[:], in_=val_pool0_bf[:].indirect(offsets[:]), func=ACT.Copy)
        inv = tile([P, HALVES], F32, "inv", "val_pool1")
        nc.vector.reciprocal(out=inv[:], in_=row_sums[:])
        turn_values(1, vg1, vt01[:, width : 2 * width])
        for h in range(HALVES):
            w = tile([P, I], BF16, "w%d" % h)
            nc.vector.scalar_tensor_tensor(
                out=w[:], in0=p_rows[h][:], scalar=inv[:, h : h + 1], in1=size_all[:], op0=ALU.mult, op1=ALU.mult
            )
            words = w[:].bitcast(F32)
            turn([words[:, block(u)] for u in range(2)], "turn%d" % h, "wt_ps%d" % h, wt[:, h * width : (h + 1) * width])
        turn_values(0, vg0, vt01[:, 0:width])
        vg2 = gather_values(2, None)
        vg3 = gather_values(3, None)
        turn_values(2, vg2, vt2[:])
        turn_values(3, vg3, vt3[:])
        w_mx = mx_tiles("w", Q, "val_pool3")
        quantise(w_mx, everything, wt[:])
        v01_mx = mx_tiles("v01", 2 * P, "wt")
        quantise(v01_mx, everything, vt01[:])
        v2_mx = mx_tiles("v2", P, "vt01")
        quantise(v2_mx, everything, vt2[:])
        v3_mx = mx_tiles("v3", P)
        quantise(v3_mx, everything, vt3[:])

        result = tile([P, PACK, Q], F32, "result")
        acc01 = ps.tile([P, 2, Q], F32, name="acc01", tag="scores0")
        for j in range(2):
            product(acc01[:, j, :], v01_mx, block(j), w_mx, everything)
        acc2 = ps.tile([P, Q], F32, name="acc2", tag="scores1")
        product(acc2[:], v2_mx, everything, w_mx, everything)
        acc3 = [ps.tile([P, P], F32, name="acc3_%d" % h) for h in range(HALVES)]
        for h in range(HALVES):
            product(acc3[h][:], v3_mx, everything, w_mx, block(h))
        nc.scalar.copy(out=result[:, 0:2, :], in_=acc01[:])
        nc.sync.dma_start(out=out_rows[:, 0:2, :], in_=result[:, 0:2, :])
        nc.vector.tensor_copy(out=result[:, 2, :], in_=acc2[:])
        nc.vector.tensor_copy(out=result[:, 3, block(0)], in_=acc3[0][:])
        nc.scalar.copy(out=result[:, 3, block(1)], in_=acc3[1][:])
        nc.sync.dma_start(out=out_rows[:, 2:4, :], in_=result[:, 2:4, :])

        y_bf = [tile([P, P, PACK], BF16, "y_bf%d" % h) for h in range(HALVES)]
        nc.vector.tensor_copy(out=weave_into(y_bf[0][:]), in_=woven(result[:, :, block(0)]))
        nc.scalar.copy(out=weave_into(y_bf[1][:]), in_=woven(result[:, :, block(1)]))
        y_mx = mx_tiles("y", Q)
        for h in range(HALVES):
            quantise(y_mx, block(h), y_bf[h][:].rearrange("p q j -> p (q j)"))
        nc.sync.dma_start(out=out_1[0].rearrange("p c r -> p (c r)").bitcast(I32), in_=y_mx[0][:].bitcast(I32))
        scale_rows = out_2[0].bitcast(I32)
        for g in range(4):
            queue = nc.scalar if g % 2 == 0 else nc.sync
            queue.dma_start(out=scale_rows[4 * g : 4 * g + 4, :], in_=y_mx[1][32 * g : 32 * g + 4, :].bitcast(I32))
